import numpy as np
import ml_dtypes

BF16 = ml_dtypes.bfloat16


def bf(x):
    return np.asarray(x, np.float32).astype(BF16)


def f32(x):
    return np.asarray(x, np.float32)


def f64(x):
    return np.asarray(x).astype(np.float64)


def striped(idx):
    return np.concatenate([l.reshape(-1, 16).T for l in idx])


def rows(idx, k):
    return np.tile(np.repeat(idx, 16, axis=0), (k // (16 * 8), 1))


def look(tab, idx):
    return np.take_along_axis(f64(tab), rows(idx, len(tab)), axis=1)


K, S, V, N, M = 512, 2048, 1024, 1024, 128


def setup_inputs():
    return {"tab": f32(np.random.standard_normal((2, K, S))), "y": f32(np.random.standard_normal((K, V))), "w": bf(np.random.standard_normal((K, M)) / np.sqrt(K)), "b": f32(0.5 * np.random.standard_normal((M, 1))), "offs": striped(np.stack([np.random.permutation(S)[:N] for _ in range(8)]))}


def reference(tab, y, w, b, offs):
    idx = np.stack([g.T.reshape(-1) for g in np.split(offs, 8)])
    x = (look(tab[0], idx) * f64(y)) * (1.0 / (1.0 + np.exp(-look(tab[1], idx))))
    return np.maximum(f64(w).T @ x + f64(b), 0.0)

@@ -1,0 +1,63 @@
+import concourse.mybir as mybir
+
+F32, BF16, U16 = mybir.dt.float32, mybir.dt.bfloat16, mybir.dt.uint16
+mult = mybir.AluOpType.mult
+sigmoid = mybir.ActivationFunctionType.Sigmoid
+relu = mybir.ActivationFunctionType.Relu
+
+P = 128
+ROWS = 512
+PLACES = 2048
+N = 1024
+M = 128
+PIECE = 512
+BLOCKS = ROWS // P
+PIECES = N // PIECE
+PIECE_OFFSETS = PIECE // 16
+
+FLOPS = 2 * ROWS * M * N
+
+
+def tile_lookup_vg_mulsig_relu_kernel(tc, tab, y, w, b, offs, out):
+    nc = tc.nc
+    with (
+        tc.tile_pool(name="held", bufs=1) as held,
+        tc.tile_pool(name="work", bufs=2) as work,
+        tc.psum_pool(name="sums", bufs=1) as sums,
+    ):
+        offsets = held.tile([P, N // 16], U16, name="offsets")
+        nc.sync.dma_start(offsets[:], offs)
+
+        weights = held.tile([P, BLOCKS, M], BF16, name="weights")
+        nc.scalar.dma_start(weights[:], w.rearrange("(k p) m -> p k m", p=P))
+        bias = held.tile([P, 1], F32, name="bias")
+        nc.scalar.dma_start(bias[:], b)
+
+        values, stream, gates = [], [], []
+        for k in range(BLOCKS):
+            rows = slice(k * P, (k + 1) * P)
+            values.append(held.tile([P, PLACES], F32, name="values%d" % k))
+            stream.append(held.tile([P, N], F32, name="stream%d" % k))
+            gates.append(held.tile([P, PLACES], F32, name="gates%d" % k))
+            nc.sync.dma_start(values[k][:], tab[0, rows, :])
+            nc.sync.dma_start(stream[k][:], y[rows, :])
+            nc.sync.dma_start(gates[k][:], tab[1, rows, :])
+
+        banks = [sums.tile([M, PIECE], F32, name="bank%d" % h) for h in range(PIECES)]
+        for k in range(BLOCKS):
+            for h in range(PIECES):
+                columns = slice(h * PIECE, (h + 1) * PIECE)
+                piece = offsets[:, h * PIECE_OFFSETS : (h + 1) * PIECE_OFFSETS]
+                product = work.tile([P, PIECE], F32, name="product")
+                gate = work.tile([P, PIECE], F32, name="gate")
+                x = work.tile([P, PIECE], BF16, name="x")
+                nc.vector.tensor_tensor(product[:], values[k][:].indirect(piece), stream[k][:, columns], mult)
+                nc.scalar.activation(gate[:], gates[k][:].indirect(piece), sigmoid)
+                nc.vector.tensor_tensor(x[:], product[:], gate[:], mult)
+                nc.tensor.matmul(banks[h][:], weights[:, k, :], x[:], start=(k == 0), stop=(k == BLOCKS - 1))
+
+        for h in range(PIECES):
+            columns = slice(h * PIECE, (h + 1) * PIECE)
+            result = held.tile([M, PIECE], F32, name="result%d" % h)
+            nc.scalar.activation(result[:], banks[h][:], relu, bias=bias[:])
+            nc.sync.dma_start(out[:, columns], result[:])

@@ -4,6 +4,7 @@ F32, BF16, U16 = mybir.dt.float32, mybir.dt.bfloat16, mybir.dt.uint16
 mult = mybir.AluOpType.mult
 sigmoid = mybir.ActivationFunctionType.Sigmoid
 relu = mybir.ActivationFunctionType.Relu
+add, larger = mybir.AluOpType.add, mybir.AluOpType.max
 
 P = 128
 ROWS = 512
@@ -11,8 +12,10 @@ PLACES = 2048
 N = 1024
 M = 128
 PIECE = 512
+STRIP = 256
 BLOCKS = ROWS // P
 PIECES = N // PIECE
+STRIPS = N // STRIP
 PIECE_OFFSETS = PIECE // 16
 
 FLOPS = 2 * ROWS * M * N
@@ -43,7 +46,7 @@ def tile_lookup_vg_mulsig_relu_kernel(tc, tab, y, w, b, offs, out):
             nc.sync.dma_start(stream[k][:], y[rows, :])
             nc.sync.dma_start(gates[k][:], tab[1, rows, :])
 
-        banks = [sums.tile([M, PIECE], F32, name="bank%d" % h) for h in range(PIECES)]
+        banks = [sums.tile([M, STRIP], F32, name="bank%d" % s) for s in range(STRIPS)]
         for k in range(BLOCKS):
             for h in range(PIECES):
                 columns = slice(h * PIECE, (h + 1) * PIECE)
@@ -53,11 +56,16 @@ def tile_lookup_vg_mulsig_relu_kernel(tc, tab, y, w, b, offs, out):
                 x = work.tile([P, PIECE], BF16, name="x")
                 nc.vector.tensor_tensor(product[:], values[k][:].indirect(piece), stream[k][:, columns], mult)
                 nc.scalar.activation(gate[:], gates[k][:].indirect(piece), sigmoid)
-                nc.vector.tensor_tensor(x[:], product[:], gate[:], mult)
-                nc.tensor.matmul(banks[h][:], weights[:, k, :], x[:], start=(k == 0), stop=(k == BLOCKS - 1))
+                for t in range(PIECE // STRIP):
+                    strip = slice(t * STRIP, (t + 1) * STRIP)
+                    bank = banks[h * (PIECE // STRIP) + t]
+                    nc.vector.tensor_tensor(x[:, strip], product[:, strip], gate[:, strip], mult)
+                    nc.tensor.matmul(bank[:], weights[:, k, :], x[:, strip], start=(k == 0), stop=(k == BLOCKS - 1))
 
-        for h in range(PIECES):
-            columns = slice(h * PIECE, (h + 1) * PIECE)
-            result = held.tile([M, PIECE], F32, name="result%d" % h)
-            nc.scalar.activation(result[:], banks[h][:], relu, bias=bias[:])
-            nc.sync.dma_start(out[:, columns], result[:])
+        for s in range(STRIPS):
+            result = held.tile([M, STRIP], F32, name="result%d" % s)
+            if s % 2 == 0:
+                nc.scalar.activation(result[:], banks[s][:], relu, bias=bias[:])
+            else:
+                nc.vector.tensor_scalar(result[:], banks[s][:], bias[:], 0.0, op0=add, op1=larger)
+            nc.sync.dma_start(out[:, s * STRIP : (s + 1) * STRIP], result[:])

@@ -4,7 +4,6 @@ F32, BF16, U16 = mybir.dt.float32, mybir.dt.bfloat16, mybir.dt.uint16
 mult = mybir.AluOpType.mult
 sigmoid = mybir.ActivationFunctionType.Sigmoid
 relu = mybir.ActivationFunctionType.Relu
-add, larger = mybir.AluOpType.add, mybir.AluOpType.max
 
 P = 128
 ROWS = 512
@@ -43,29 +42,27 @@ def tile_lookup_vg_mulsig_relu_kernel(tc, tab, y, w, b, offs, out):
             stream.append(held.tile([P, N], F32, name="stream%d" % k))
             gates.append(held.tile([P, PLACES], F32, name="gates%d" % k))
             nc.sync.dma_start(values[k][:], tab[0, rows, :])
-            nc.sync.dma_start(stream[k][:], y[rows, :])
+            ahead = N if k < BLOCKS - 1 else N // 2
+            nc.sync.dma_start(stream[k][:, :ahead], y[rows, :ahead])
             nc.sync.dma_start(gates[k][:], tab[1, rows, :])
+        nc.sync.dma_start(stream[k][:, ahead:], y[rows, ahead:])
 
         banks = [sums.tile([M, STRIP], F32, name="bank%d" % s) for s in range(STRIPS)]
         for k in range(BLOCKS):
+            product = work.tile([P, N], F32, name="product")
+            gate = work.tile([P, N], F32, name="gate")
+            x = work.tile([P, N], BF16, name="x")
             for h in range(PIECES):
                 columns = slice(h * PIECE, (h + 1) * PIECE)
                 piece = offsets[:, h * PIECE_OFFSETS : (h + 1) * PIECE_OFFSETS]
-                product = work.tile([P, PIECE], F32, name="product")
-                gate = work.tile([P, PIECE], F32, name="gate")
-                x = work.tile([P, PIECE], BF16, name="x")
-                nc.vector.tensor_tensor(product[:], values[k][:].indirect(piece), stream[k][:, columns], mult)
-                nc.scalar.activation(gate[:], gates[k][:].indirect(piece), sigmoid)
-                for t in range(PIECE // STRIP):
-                    strip = slice(t * STRIP, (t + 1) * STRIP)
-                    bank = banks[h * (PIECE // STRIP) + t]
-                    nc.vector.tensor_tensor(x[:, strip], product[:, strip], gate[:, strip], mult)
-                    nc.tensor.matmul(bank[:], weights[:, k, :], x[:, strip], start=(k == 0), stop=(k == BLOCKS - 1))
+                nc.vector.tensor_tensor(product[:, columns], values[k][:].indirect(piece), stream[k][:, columns], mult)
+                nc.scalar.activation(gate[:, columns], gates[k][:].indirect(piece), sigmoid)
+            for s in range(STRIPS):
+                strip = slice(s * STRIP, (s + 1) * STRIP)
+                nc.vector.tensor_tensor(x[:, strip], product[:, strip], gate[:, strip], mult)
+                nc.tensor.matmul(banks[s][:], weights[:, k, :], x[:, strip], start=(k == 0), stop=(k == BLOCKS - 1))
 
         for s in range(STRIPS):
             result = held.tile([M, STRIP], F32, name="result%d" % s)
-            if s % 2 == 0:
-                nc.scalar.activation(result[:], banks[s][:], relu, bias=bias[:])
-            else:
-                nc.vector.tensor_scalar(result[:], banks[s][:], bias[:], 0.0, op0=add, op1=larger)
+            nc.scalar.activation(result[:], banks[s][:], relu, bias=bias[:])
             nc.sync.dma_start(out[:, s * STRIP : (s + 1) * STRIP], result[:])

@@ -11,7 +11,7 @@ PLACES = 2048
 N = 1024
 M = 128
 PIECE = 512
-STRIP = 256
+STRIP = 128
 BLOCKS = ROWS // P
 PIECES = N // PIECE
 STRIPS = N // STRIP

import concourse.mybir as mybir

F32, BF16, U16 = mybir.dt.float32, mybir.dt.bfloat16, mybir.dt.uint16
mult = mybir.AluOpType.mult
sigmoid = mybir.ActivationFunctionType.Sigmoid
relu = mybir.ActivationFunctionType.Relu

P = 128
ROWS = 512
PLACES = 2048
N = 1024
M = 128
PIECE = 512
STRIP = 128
BLOCKS = ROWS // P
PIECES = N // PIECE
STRIPS = N // STRIP
PIECE_OFFSETS = PIECE // 16

FLOPS = 2 * ROWS * M * N


def tile_lookup_vg_mulsig_relu_kernel(tc, tab, y, w, b, offs, out):
    nc = tc.nc
    with (
        tc.tile_pool(name="held", bufs=1) as held,
        tc.tile_pool(name="work", bufs=2) as work,
        tc.psum_pool(name="sums", bufs=1) as sums,
    ):
        offsets = held.tile([P, N // 16], U16, name="offsets")
        nc.sync.dma_start(offsets[:], offs)

        weights = held.tile([P, BLOCKS, M], BF16, name="weights")
        nc.scalar.dma_start(weights[:], w.rearrange("(k p) m -> p k m", p=P))
        bias = held.tile([P, 1], F32, name="bias")
        nc.scalar.dma_start(bias[:], b)

        values, stream, gates = [], [], []
        for k in range(BLOCKS):
            rows = slice(k * P, (k + 1) * P)
            values.append(held.tile([P, PLACES], F32, name="values%d" % k))
            stream.append(held.tile([P, N], F32, name="stream%d" % k))
            gates.append(held.tile([P, PLACES], F32, name="gates%d" % k))
            nc.sync.dma_start(values[k][:], tab[0, rows, :])
            ahead = N if k < BLOCKS - 1 else N // 2
            nc.sync.dma_start(stream[k][:, :ahead], y[rows, :ahead])
            nc.sync.dma_start(gates[k][:], tab[1, rows, :])
        nc.sync.dma_start(stream[k][:, ahead:], y[rows, ahead:])

        banks = [sums.tile([M, STRIP], F32, name="bank%d" % s) for s in range(STRIPS)]
        for k in range(BLOCKS):
            product = work.tile([P, N], F32, name="product")
            gate = work.tile([P, N], F32, name="gate")
            x = work.tile([P, N], BF16, name="x")
            for h in range(PIECES):
                columns = slice(h * PIECE, (h + 1) * PIECE)
                piece = offsets[:, h * PIECE_OFFSETS : (h + 1) * PIECE_OFFSETS]
                nc.vector.tensor_tensor(product[:, columns], values[k][:].indirect(piece), stream[k][:, columns], mult)
                nc.scalar.activation(gate[:, columns], gates[k][:].indirect(piece), sigmoid)
            for s in range(STRIPS):
                strip = slice(s * STRIP, (s + 1) * STRIP)
                nc.vector.tensor_tensor(x[:, strip], product[:, strip], gate[:, strip], mult)
                nc.tensor.matmul(banks[s][:], weights[:, k, :], x[:, strip], start=(k == 0), stop=(k == BLOCKS - 1))

        for s in range(STRIPS):
            result = held.tile([M, STRIP], F32, name="result%d" % s)
            nc.scalar.activation(result[:], banks[s][:], relu, bias=bias[:])
            nc.sync.dma_start(out[:, s * STRIP : (s + 1) * STRIP], result[:])
